import numpy as np, ml_dtypes
CORES = [66,74,82,90,194,202,210,218]
N = 8
import mx_ref
BF = ml_dtypes.bfloat16
def gentries(a):
    return np.ascontiguousarray(a.reshape(8, 16, -1).transpose(0, 2, 1)).reshape(8, -1)
def gtable(e):
    e = np.asarray(e); return np.ascontiguousarray(e.reshape(8, -1, 16).transpose(0, 2, 1)).reshape(128, -1).astype(np.int32)
def gcols(t, e):
    v = np.concatenate([t.reshape(8, 16, -1, 4), np.zeros((8, 16, 1, 4), BF)], axis=2)
    return np.ascontiguousarray(np.stack([v[g][:, e[g]] for g in range(8)])).reshape(128, -1)
def gpick(z, e):
    return np.concatenate([z[16 * g:16 * g + 16][:, e[g]] for g in range(8)])
def tile(rs):
    return np.stack(rs, axis=2).reshape(128, -1).astype(BF)
def pick(q, e):
    c = np.concatenate([q[0].reshape(128, -1, 4), np.zeros((128, 1, 4), np.uint8)], axis=1); s = np.concatenate([q[1], np.ones((16, 1), np.uint8)], axis=1)
    return (np.ascontiguousarray(c[:, e].reshape(128, -1)), np.ascontiguousarray(s[:, e]))
def join(*qs):
    return (np.concatenate([q[0] for q in qs], axis=1), np.concatenate([q[1] for q in qs], axis=1))
def put(q, e, v):
    c, s = q[0].reshape(128, -1, 4).copy(), q[1].copy(); c[:, e] = v[0].reshape(128, -1, 4); s[:, e] = v[1]
    return (c.reshape(128, -1), s)
def pk(c, s):
    return (np.ascontiguousarray(c), mx_ref.live(s))
def emit(q):
    return q[0], q[1]
def packed(v, rng):
    q = [mx_ref.quantize(np.ascontiguousarray(v[r])) for r in range(N)]
    return np.stack([a for a, b in q]), np.stack([mx_ref.plane(b, rng) for a, b in q])
def values_of_codes():
    e, c = np.zeros((128, 128, 4), np.float32), np.zeros((128, 2, 4), np.uint8)
    e[np.arange(128), np.arange(128), 0] = 1
    c[:127, :, 0] = np.arange(256).reshape(2, 128).T[:127]
    return mx_ref.matmul(mx_ref.quantize(e.reshape(128, 512).astype(BF)), (c.reshape(128, 8), np.full((16, 2), 127, np.uint8))).T.reshape(-1).astype(np.float64)
CODE_VALUE, SCALE_VALUE = values_of_codes(), 2.0 ** (np.arange(256) - 127.0)
def decode(q):
    return (CODE_VALUE[q[0]].reshape(16, 8, -1, 4) * SCALE_VALUE[q[1]][:, None, :, None] + 0.0).reshape(128, -1).astype(np.float32)
def f(rng, *shape):
    return mx_ref.flush((rng.standard_normal(shape, dtype=np.float32) * np.exp2(rng.integers(-2, 3, shape[:-1] + (1,)))).astype(BF))
def wide(rng, *shape, cols=0):
    v = rng.standard_normal(shape, dtype=np.float32) * np.exp2(rng.integers(-12, 13, shape)).astype(np.float32)
    if cols: v *= np.repeat(np.exp2(rng.integers(-cols, cols + 1, shape[:-2] + (1, shape[-1] // 4))) * (rng.random(shape[:-2] + (1, shape[-1] // 4)) > 0.0625), 4, axis=-1).astype(np.float32)
    return mx_ref.flush(v.astype(BF))
C = 288
STEP = [4, 1, 2]
def numbers_of(rng):
    return {"x": np.array(f(rng, N, 128, 4 * C)), "u": np.array(f(rng, N, 128, 512)), "v": np.array(f(rng, N, 128, 512))}
def orders(rng):
    return rng.permuted(np.tile(np.arange(C), (N, 8, 1)), axis=2), rng.permuted(np.tile(np.arange(8)[:, None], (N, 1, C)), axis=1)
def stored(p, o):
    return {"pg": np.stack([gtable(p[r]) for r in range(N)]), "og": np.stack([gtable(o[r]) for r in range(N)])}
def layers(rng, still=[]):
    w = np.array(f(rng, N, 128, 2048)).reshape(N, 8, 16, 4, 8, 16, 4)
    for i in still:
        w[:, :, i] = 0
        w[:, :, :, :, :, i] = 0
    return w
def weights(rng, w):
    c, s = packed(np.ascontiguousarray(w).reshape(N, 128, 2048), rng)
    return {"wc": c, "ws": s}
def setup_inputs(rng):
    return {**numbers_of(rng), **stored(*orders(rng)), **weights(rng, layers(rng))}
def setup_inputs_ties(rng):
    d = numbers_of(rng)
    n = rng.permutation(N)
    k = rng.integers(0, 4, (N, 8, C))
    k[n[1]] -= 4
    k[n[2]] = np.arange(8)[:, None]
    x = d["x"].reshape(N, 8, 16, C, 4)
    x[:, :, 0] = 0
    x[:, :, 0, :, 0] = k.astype(np.float32).astype(BF)
    u = d["u"].reshape(N, 128, 128, 4)
    u[:, :, ::16] = 0
    for r in range(N):
        for h in range(0, 128, 16): u[r, h, h, 0] = 0.0 if r == n[0] else 1.0
    p, o = orders(rng)
    o[n[2]] = 7 - np.arange(8)[:, None]
    return {"x": x.reshape(N, 128, 4 * C), "u": u.reshape(N, 128, 512), "v": d["v"], **stored(p, o), **weights(rng, layers(rng, [0]))}
def setup_inputs_near(rng):
    d = numbers_of(rng)
    x = d["x"].astype(np.float32).reshape(N, 8, 16, C, 4)
    x[:, :, 0] = 0
    x[:, :, 8:] = 0
    u = d["u"].reshape(N, 128, 128, 4)
    u[:, :, ::16] = 0
    w = layers(rng, [0, 8, 9, 10, 11, 12, 13, 14, 15])
    kind, size, least = np.zeros(N, np.int64), np.ones(N), 2.0 ** -30
    turn = rng.integers(2)
    for i, r in enumerate(rng.permutation([r for r in range(N) if r < r ^ STEP[0]])):
        both = [r, r ^ STEP[0]]
        kind[both] = 2 if i == 0 else rng.permutation(2)
        size[both] = least if (i + turn) % 2 else 1.0
    for r in range(N):
        s = rng.integers(0, 16, (8, C))
        digits = ((s[:, :, None] >> np.arange(4)) & 1) * np.exp2(np.arange(4) - 23.0)
        if kind[r] == 0:
            x[r, :, 0, :, 0] = rng.choice([-1.0, 1.0])
            x[r, :, 8] = digits
            x[r, :, 11, :, 0] = 2.0 ** -10
        if kind[r] == 1: x[r, :, 8] = digits * rng.choice([-1.0, 1.0], (8, C, 1))
        if kind[r] == 2:
            e = rng.integers(-1, 2, (8, C)) * least
            x[r, :, 8, :, 0] = 1.25 * e
            x[r, :, 9, :, 0] = -1.125 * e
            x[r, :, 13, :, 0] = rng.choice([-1.0, 1.0], (8, C)) * least
            for g in range(8): w[r, g, 13, 0, g, 12, 0] = 2.0 ** -8
        for g, j in zip(rng.permutation(8)[:4], [0, C - 1, int(rng.integers(C)), int(rng.integers(C))]): x[r, g, 0, j, 0] = 2.0 ** 29 * rng.choice([-1.0, 1.0])
        k = size[r] if kind[r] == 0 else least
        for h in range(0, 128, 16):
            u[r, h, h, 0] = k if kind[r] == 0 else 1.0
            if kind[r] == 0: u[r, h + 11, h, 0] = k
            if kind[r] < 2: u[r, h + 8, h] = k
            else:
                u[r, h + 8, h, 0] = k
                u[r, h + 9, h, 0] = 1.125 * k
                u[r, h + 12, h, 0] = k
    return {"x": x.reshape(N, 128, 4 * C).astype(BF), "u": u.reshape(N, 128, 512), "v": d["v"], **stored(*orders(rng)), **weights(rng, w)}
def setup_inputs_odd(rng):
    d = numbers_of(rng)
    x = (1.0 + (2 * rng.integers(0, 64, (N, 16, 8, C, 4)) + 1) * 2.0 ** -7) * np.exp2(-rng.integers(0, 7, (N, 16, 8, C, 4)).astype(np.float64)) * rng.choice([-1.0, 1.0], (N, 16, 8, C, 4))
    x[:, :, 0, :, 0] = 1.96875 * 2.0 ** 8 * rng.choice([-1.0, 1.0], (16, 1))
    u = d["u"].reshape(N, 16, 8, 128, 4)
    u[:, :, 0, ::16] = 0
    w = layers(rng, [0, 8])
    for g in range(8):
        for i in (0, 8): w[:, g, i, 0, g, i, 0] = -0.5
    return {"x": x.astype(np.float32).reshape(N, 128, 4 * C).astype(BF), "u": u.reshape(N, 128, 512), "v": d["v"], **stored(*orders(rng)), **weights(rng, w)}
def setup_inputs_ends(rng):
    d = numbers_of(rng)
    n, e, c = [rng.permutation(N) % 4 for _ in range(3)]
    low, tiny = 2.0 ** 29, 2.0 ** -30
    def small(*s): return (1 + 0.125 * rng.integers(0, 8, s)) * tiny
    x = np.zeros((N, 8, 16, C, 4))
    u = d["u"].astype(np.float32).reshape(N, 8, 16, 128, 4)
    v = d["v"].astype(np.float32)
    w = np.zeros((N, 128, 4, 128, 4), np.float32)
    i = np.arange(128)
    p, o = orders(rng)
    for r in range(N):
        h = rng.permutation(8)
        a = np.where(h < 2, 0.0, h % 2 * 2.0 - 1.0)[:, None]
        k = np.full(16, 4.0)
        k[15] = 0
        if n[r] < 2:
            x[r] = -(1 + 0.125 * rng.integers(0, 4, (8, 16, C, 4))) * low
            if n[r] == 1: x[r] *= rng.choice([-1.0, 1.0], (C, 1))
            x[r, :, 15] = 2.0 ** 16 * rng.choice([-1.0, 1.0], (8, C, 4))
            u[r, :, :, ::16] = a * 2.0 ** 30
            v[r] = rng.choice([-1.0, 1.0], (128, 512)) * (1 + 0.125 * rng.integers(4, 9, (128, 512))) * low
        elif n[r] == 2:
            x[r] = -small(8, 16, C, 4)
            u[r, :, :, ::16] = a * small(8, 16, 8, 4)
            u[r, :, 14:, ::16] = 0
            v[r] = rng.choice([-1.0, 1.0], (128, 512)) * small(128, 512)
            k[:] = 0
            k[14], k[15] = 2.0 ** -8, 2.0 ** 8
        else:
            x[r] = d["x"][r].astype(np.float32).reshape(8, 16, C, 4)[:, :, :1]
            u[r, :, :, ::16] *= np.abs(a).astype(np.float32)
        for b in range(4): w[r, i, b, i, b] = np.tile(k, 8)
        if e[r] < 3: p[r] = [np.arange(C), np.arange(C)[::-1], (np.arange(C) + 1) % C][e[r]]
        up = np.arange(8)[:, None]
        if c[r] < 3: o[r] = np.where([np.ones(C, bool), np.zeros(C, bool), rng.random(C) < 0.5][c[r]], up, 7 - up)
    return {"x": x.astype(np.float32).reshape(N, 128, 4 * C).astype(BF), "u": u.reshape(N, 128, 512).astype(BF), "v": v.astype(BF), **stored(p, o), **weights(rng, w.astype(BF))}
def setup_inputs_spread(rng):
    d = setup_inputs(rng)
    d["x"] = wide(rng, N, 128, 4 * C, cols=6)
    return d
def check_inputs(d):
    b = []
    for k in ("x", "u", "v"):
        a = np.abs(d[k].astype(np.float32))
        if not (np.isfinite(a).all() and ((a == 0) | (a >= 2.0 ** -30) & (a <= 2.0 ** 30)).all()): b.append("a value of " + k)
    none, least, most = [emit(mx_ref.quantize(np.full((128, 16), k, np.float32).astype(BF)))[1][0, 0] for k in (0.0, 2.0 ** -8, 2.0 ** 8)]
    for r in range(N):
        if not (np.sort(gentries(d["pg"][r]), axis=1) == np.arange(C)).all(): b.append("pg: a group's entries aren't all columns")
        if not (np.sort(gentries(d["og"][r]), axis=0) == np.arange(8)[:, None]).all(): b.append("og: a column's entries aren't all groups")
        if ((d["wc"][r] == 0x7F) | (d["wc"][r] == 0xFF)).any(): b.append("wc: a code that is no number")
        s = mx_ref.live(d["ws"][r])
        if ((s != none) & ((s < least) | (s > most))).any(): b.append("ws: a scale out of range")
        if (((d["wc"][r].reshape(16, 8, 512, 4) & 0x7F) != 0) & (s == none)[:, None, :, None]).any(): b.append("wc: a code other than zero under the scale of zeros")
    return b
def walk(p, o):
    a, at = np.arange(C), np.zeros((8, C), np.int64)
    for k in range(8):
        a = p[o[k], a]
        at[o[k], np.arange(C)] = a
    return at
def reference(x, u, v, pg, og, wc, ws):
    qu = [mx_ref.quantize(u[r]) for r in range(N)]
    lay = [pk(wc[r], ws[r]) for r in range(N)]
    p, o = [np.array(gentries(pg[r])) for r in range(N)], [np.array(gentries(og[r])) for r in range(N)]
    at = [walk(p[r], o[r]) for r in range(N)]
    now = [x[r] for r in range(N)]
    for t, step in enumerate(STEP):
        held, z = [], []
        for r in range(N):
            q = mx_ref.quantize(now[r])
            held.append(decode(q))
            s = mx_ref.matmul(qu[r], q)[::16]
            c = s[o[r], at[r][o[r], np.arange(C)]]
            for k in range(t % 2, 7, 2):
                turn = c[k] > c[k + 1]
                o[r][k], o[r][k + 1] = np.where(turn, o[r][k + 1], o[r][k]), np.where(turn, o[r][k], o[r][k + 1])
            at[r] = walk(p[r], o[r])
            z.append(mx_ref.quantize(gcols(held[r].astype(BF), at[r])))
        for r in range(N):
            e = np.take_along_axis(p[r], at[r], axis=1)
            now[r] = tile([held[r][:, b::4] + gpick(mx_ref.matmul(pick(lay[r], np.arange(128 * b, 128 * b + 128)), z[r ^ step]) * np.float32(0.03125), e) for b in range(4)])
    y, ol = np.zeros((N, 128, C), np.float32), np.zeros((N, 8, C), np.float32)
    oc, osc = np.zeros((N, 128, 4 * C), np.uint8), np.zeros((N, 16, C), np.uint8)
    for r in range(N):
        q = mx_ref.quantize(now[r])
        y[r] = mx_ref.matmul(mx_ref.quantize(v[r]), q)
        ol[r] = o[r]
        oc[r], osc[r] = emit(q)
    return {"y": y, "ol": ol, "oc": oc, "osc": osc}

@@ -1,0 +1,354 @@
+from concourse.mybir import dt, AluOpType, ActivationFunctionType
+
+STEP = (4, 1, 2)
+NB = 9
+BL = 9
+
+
+def blk(k):
+    return k // 2 if k % 2 == 0 else 5 + k // 2
+
+
+BF, F32, I32, U16, F16 = "bfloat16", "float32", "int32", "uint16", "float16"
+SCRATCH = {}
+for _d, _names in (
+        (BF, "diag 384 keepb 384 keepl 288 et 2048 lt 512 ut 512 vt 512 pt 2304 gm 2592 oh 162 fg 288 ft 288 gb 288 sb 288 xb 512 "
+             "f0 288 f1 288 f2 288 f3 288 d0 288 d1 288 d2 288 d3 288 x0 1152 x1 1152 x2 1152 x3 1152 z0 1152 z1 1152 z2 1152"),
+        (F32, "pf 8 keepf 384 jm 9 o 81 od 72 dd 36 mm 36 ab 162 dv 72 sov 72 sw 2304 ge 384 ee 384 ok 96 ot 96 yt 288 "
+              "r0 288 r1 288 r2 288 r3 288"),
+        (I32, "pi 8 io 128 ioa 128 ip 384 ipa 384 ie 384 iea 384 ieb 384 ji 9 cli 144 uli 64 raw 2304 oi 144"),
+        (U16, "cl 144 ul 64 uo 90 uf 18 ub 18 so 24 al0 18 al1 18 al2 18 bl0 18 bl1 18 bl2 18 ll0 18 ll1 18 ll2 18"),
+        (F16, "sc 2592 pm 162 p1 72 p2 36 p3 18")):
+    _w = _names.split()
+    for _n, _c in zip(_w[0::2], _w[1::2]):
+        SCRATCH[_n] = ("sbuf", [128, int(_c)], _d)
+for _n, _c in (("e", 512), ("l", 128), ("u", 128), ("r", 1024), ("v", 128), ("w", 512), ("b", 128)) + tuple(
+        (_m, 288) for _m in ("x0", "x1", "x2", "x3", "p0", "p1", "p2", "z0", "z1", "z2")):
+    SCRATCH["C" + _n], SCRATCH["S" + _n] = ("sbuf", [128, _c], "float8_e4m3fn_x4"), ("sbuf", [128, _c], "uint8")
+SCRATCH["old"] = ("dram", [72, 32], F32)
+for _b in range(8):
+    SCRATCH["ps%d" % _b] = ("psum", [128, 512], F32)
+SEMAPHORES = ["vq_", "sq_", "tq_", "gq_"] + ["dm%d" % i for i in range(16)] + [
+    n + str(t) for t in range(3) for n in ("ca", "cb", "sa", "sb", "la", "lb")]
+
+
+def rank_program(g, core, T, topo):
+    rank = T.rank_of(core)
+    if rank is None:
+        return
+    A, AF = AluOpType, ActivationFunctionType
+    queue = {"v": g.vector, "s": g.scalar, "t": g.tensor, "g": g, "y": g.sync}
+    known = {e: {} for e in queue}
+    total, waited, snap, recs = {}, {}, {}, {}
+
+    def L(name, lo, n, st=1, p0=0, p1=128):
+        return (name, lo, lo + st * (n - 1) + 1, st, p0, p1)
+
+    def W(name):
+        return (name, 0, SCRATCH[name][1][1], 1, 0, 128)
+
+    def ap(v, idx=None):
+        name, lo, hi, st, p0, p1 = v
+        a = T[name][p0:p1, lo:hi] if st == 1 else T[name][p0:p1, lo:hi:st]
+        return a.indirect(ap(idx)) if idx else a
+
+    def u8(v):
+        return ap(v).bitcast(dt.uint8)
+
+    def clash(a, b):
+        if a[0].startswith("ps"):
+            return True
+        if a[1] >= b[2] or b[1] >= a[2] or a[4] >= b[5] or b[4] >= a[5]:
+            return False
+        return not (a[3] == b[3] and a[3] > 1 and (a[1] - b[1]) % a[3])
+
+    def need(e, reads, writes, asyn=False):
+        want = {}
+        for acc, w in [(r, False) for r in reads] + [(r, True) for r in writes]:
+            for e2, sem, val, w2, acc2 in recs.get(acc[0], []):
+                if not (w or w2 or acc[0].startswith("ps")) or not clash(acc, acc2):
+                    continue
+                if e2 == e and not asyn and not w2:
+                    continue
+                if val > known[e].get(sem, 0):
+                    want[sem] = max(want.get(sem, 0), val)
+        for sem, val in sorted(want.items(), key=lambda kv: -kv[1]):
+            if known[e].get(sem, 0) >= val:
+                continue
+            queue[e].wait_ge(T.sem[sem], val)
+            waited[sem] = max(waited.get(sem, 0), val)
+            known[e][sem] = val
+            for s2, v2 in snap.get((sem, val), {}).items():
+                known[e][s2] = max(known[e].get(s2, 0), v2)
+
+    def note(e2, sem, val, reads, writes):
+        for acc in writes:
+            recs[acc[0]] = [r for r in recs.get(acc[0], []) for b in [r[4]] if not (
+                acc[1] <= b[1] and b[2] <= acc[2] and acc[4] <= b[4] and b[5] <= acc[5]
+                and (acc[3] == 1 or (acc[3] == b[3] and (acc[1] - b[1]) % acc[3] == 0)))]
+        for acc, w in [(r, False) for r in reads] + [(r, True) for r in writes]:
+            recs.setdefault(acc[0], []).append((e2, sem, val, w, acc))
+
+    def do(e, call, reads, writes):
+        need(e, reads, writes)
+        sem = e + "q_"
+        total[sem] = total.get(sem, 0) + 1
+        call().then_inc(T.sem[sem], 1)
+        snap[(sem, total[sem])] = dict(known[e])
+        note(e, sem, total[sem], reads, writes)
+
+    nd = [0]
+
+    def dmas(jobs):
+        sem = "dm%d" % nd[0]
+        nd[0] += 1
+        total[sem] = 16 * len(jobs)
+        k = {}
+        for e, out, in_, reads, writes in jobs:
+            need(e, reads, writes, True)
+            queue[e].dma_start(out, in_).then_inc(T.sem[sem], 16)
+            for s2, v2 in known[e].items():
+                k[s2] = max(k.get(s2, 0), v2)
+        snap[(sem, total[sem])] = k
+        for e, out, in_, reads, writes in jobs:
+            note("dma", sem, total[sem], reads, writes)
+
+    def send(dst, out, in_, arr, loc, code=False):
+        need("g", [in_], [], True)
+        rid, pid = topo.addr(dst, core)
+        n = len(topo.engines(core, dst))
+        f = u8 if code else ap
+        g.remote_dma(f(out), f(in_), T.sem[arr], T.sem[loc], pid, rid, topo.mask(core, dst))
+        total[arr] = total[loc] = n
+        snap[(loc, n)] = dict(known["g"])
+        note("dma", loc, n, [in_], [])
+        note("dma", arr, n, [], [out])
+
+    def more(*vs):
+        return [v for v in vs if isinstance(v, tuple)]
+
+    def tt(out, a, b, op, idx=None):
+        do("v", lambda: g.vector.tensor_tensor(ap(out), ap(a, idx), ap(b), op), [a, b] + more(idx), [out])
+
+    def ts(out, a, s1, op0, s2=None, op1=None, idx=None):
+        c = [ap(s) if isinstance(s, tuple) else s for s in (s1, s2)]
+        ops = (op0,) if op1 is None else (op0, op1)
+        do("v", lambda: g.vector.tensor_scalar(ap(out), ap(a, idx), c[0], c[1], *ops), [a] + more(s1, s2, idx), [out])
+
+    def copy(out, a, idx=None):
+        do("v", lambda: g.vector.tensor_copy(ap(out), ap(a, idx)), [a] + more(idx), [out])
+
+    def scan(out, d0, d1):
+        do("v", lambda: g.vector.tensor_tensor_scan(ap(out), ap(d0), ap(d1), 0.0, A.mult, A.add), [d0, d1], [out])
+
+    def turn(out, a):
+        do("v", lambda: g.vector.transpose(ap(out), ap(a)), [a], [out])
+
+    def act(out, a, func, idx=None, **kw):
+        k2 = {k: ap(v) if isinstance(v, tuple) else v for k, v in kw.items()}
+        do("s", lambda: g.scalar.activation(ap(out), ap(a, idx), func, **k2), [a] + more(idx, *kw.values()), [out])
+
+    def quant(n, name, x):
+        q, s, v = L("C" + name, 0, n), L("S" + name, 0, n), L(x, 0, 4 * n)
+        do("v", lambda: g.vector.quantize_mx(ap(q), ap(s), ap(v)), [v], [q, s])
+
+    def mm(bank, n, w, w0, x, x0=0):
+        a, b, c, d = L("C" + w, w0, 128), L("S" + w, w0, 128), L("C" + x, x0, n), L("S" + x, x0, n)
+        o = L("ps%d" % bank, 0, n)
+        do("t", lambda: g.tensor.matmul_mx(ap(o), ap(a), ap(b), ap(c), ap(d), True, True), [a, b, c, d], [o])
+
+    def fill(v, k):
+        do("v", lambda: g.vector.memset(ap(v), k), [], [v])
+
+    def iota(v, pattern, base, cm):
+        do("g", lambda: g.iota(ap(v), pattern, base, cm), [], [v])
+
+    q2 = ("y", "s")
+    dmas([(q2[r % 2], T.raw[r:r + 1, :], T.pg[:, :], [], [L("raw", 0, 2304, 1, r, r + 1)]) for r in range(16)])
+    dmas([(q2[k % 2], T.oi[0:16, c:c + 18], T.og[16 * k:16 * k + 16, :], [], [L("oi", c, 18, 1, 0, 16)])
+          for k in range(8) for c in [18 * (k // 2 + 4 * (k % 2))]])
+    dmas([("y", T.x0[:, :], T.x[:, :], [], [W("x0")])])
+    dmas([("s", T.ut[:, :], T.u[:, :], [], [W("ut")])])
+    iota(L("pi", 0, 1), [[0, 1]], 0, 1)
+    iota(W("uli"), [[16, 8], [0, 8]], 0, 0)
+    iota(W("io"), [[-1, 128]], 128, 1)
+    iota(W("ip"), [[-1, 384]], 384, 1)
+    iota(W("ie"), [[1, 384]], 0, 0)
+    iota(W("ji"), [[32, NB]], -144, 0)
+    iota(W("cli"), [[288, 8], [1, 18]], 0, 0)
+    for name, n in (("raw", 2304), ("oi", 144)):
+        dmas([(q2[h % 2], T[name][16 * h:16 * h + 16, :], T[name][0:16, :], [L(name, 0, n, 1, 0, 16)], [L(name, 0, n, 1, 16 * h, 16 * h + 16)])
+              for h in range(1, 8)])
+    dmas([("y", u8(W("Cw")), T.wc[:, :], [], [W("Cw")]), ("y", T.Sw[:, :], T.ws[:, :], [], [W("Sw")]), ("y", T.vt[:, :], T.v[:, :], [], [W("vt")])])
+
+    copy(W("ul"), W("uli"))
+    fill(W("et"), 0.0)
+    fill(W("lt"), 0.0)
+    for b in range(4):
+        ts(L("et", 512 * b + b, 128, 4), W("io"), 128, A.is_equal)
+    ts(W("ioa"), W("io"), 31, A.bitwise_and)
+    ts(L("lt", 0, 128, 4), W("ioa"), 0, A.is_equal)
+    quant(512, "e", "et")
+    quant(128, "l", "lt")
+    ts(W("ipa"), W("ip"), 15, A.bitwise_and)
+    ts(W("diag"), W("ipa"), 0, A.is_equal)
+    ts(W("iea"), W("ie"), 15, A.bitwise_and)
+    ts(W("ieb"), W("ie"), 31, A.bitwise_and)
+    ts(W("keepf"), W("iea"), 0, A.is_gt)
+    ts(W("keepb"), W("iea"), 0, A.is_gt)
+    ts(W("keepl"), L("ieb", 0, 288), 0, A.is_gt)
+    P = lambda j: L("pi", j, 1)
+    Q = lambda j: L("pf", j, 1)
+    ts(P(1), P(0), 15, A.bitwise_and)
+    ts(P(2), P(0), 31, A.bitwise_and)
+    ts(P(3), P(0), 4, A.arith_shift_right)
+    ts(P(4), P(0), 5, A.arith_shift_right)
+    ts(P(5), P(3), 1, A.bitwise_and)
+    ts(Q(1), P(1), 18, A.mult)
+    ts(Q(2), P(2), 0, A.add)
+    ts(Q(3), P(3), 288, A.mult, 144, A.add)
+    ts(Q(4), P(4), -2, A.mult)
+    ts(Q(5), P(4), -2, A.mult, -1, A.add)
+    ts(Q(6), P(5), 0, A.add)
+    ts(W("jm"), W("ji"), Q(2), A.add)
+    ts(W("cl"), W("cli"), Q(1), A.add)
+    fill(W("gm"), 0.0)
+    fill(W("xb"), 0.0)
+    fill(L("ok", 72, 24), 0.0)
+    fill(L("o", 36, 9), 8.0)
+    quant(128, "u", "ut")
+    do("v", lambda: g.vector.tensor_copy(ap(W("Cr")).bitcast(dt.uint32), ap(W("Cu")).bitcast(dt.uint32).indirect(ap(W("ul")))),
+       [W("Cu"), W("ul")], [W("Cr")])
+    act(W("Sr"), W("Su"), AF.Copy, idx=W("ul"))
+
+    EV, OD = 0, 45
+    base = lambda b0, n: L("gm", 288 * b0 + 1, NB * n, 32)
+    last = lambda b0, n: L("sc", 288 * b0 + 31, NB * n, 32)
+    off = lambda k: L("uo", 10 * k, NB)
+
+    def step(k):
+        s = blk(k)
+        tt(L("gm", 288 * s, 144, 2), W("pt"), L("diag", 0, 144), A.mult, idx=off(k - 1))
+        scan(L("sc", 288 * s, 288), W("keepl"), L("gm", 288 * s, 288))
+
+    def walk():
+        ts(base(0, BL), W("o"), 288, A.mult, -1152, A.add)
+        tt(last(0, 1), base(0, 1), W("jm"), A.add)
+        ts(off(0), last(0, 1), 1296, A.add)
+        for k in range(1, 8):
+            step(k)
+            ts(off(k), last(blk(k), 1), 1296, A.add)
+
+    def score_lists(t):
+        step(8)
+        tt(W("dv"), last(1, 8), base(1, 8), A.subtract)
+        tt(L("sov", 0, 36), L("dv", 36, 36), base(0, 4), A.add)
+        tt(L("sov", 36, 36), L("dv", 0, 36), base(5, 4), A.add)
+        for a, (p0, p1) in enumerate(((0, 32), (32, 64), (64, 128))):
+            ts(L("so", 0, 24, 1, p0, p1), L("sov", a, 24, 3, p0, p1), 1296, A.add)
+        if t % 2 == 0:
+            tt(L("dd", 0, 36), L("o", OD, 36), L("o", EV, 36), A.subtract)
+        else:
+            tt(L("dd", 0, 27), L("o", EV + 9, 27), L("o", OD, 27), A.subtract)
+
+    def products(t):
+        x = "x%d" % t
+        quant(288, x, x)
+        if t == 3:
+            return
+        dst = T.cores[rank ^ STEP[t]]
+        send(dst, W("Cp%d" % t), W("C" + x), "ca%d" % t, "cb%d" % t, True)
+        send(dst, W("Sp%d" % t), W("S" + x), "sa%d" % t, "sb%d" % t)
+        for i in range(8):
+            mm(i, 288, "r", 128 * i, x)
+            if i % 2 == 0:
+                copy(L("sw", 288 * i, 288), L("ps%d" % i, 0, 288))
+            else:
+                act(L("sw", 288 * i, 288), L("ps%d" % i, 0, 288), AF.Copy)
+        for b in range(4):
+            mm(b, 288, "e", 128 * b, x)
+            act(W("f%d" % b), L("ps%d" % b, 0, 288), AF.Copy)
+
+    products(0)
+    tt(W("od"), L("oi", 1, 72, 2), L("oi", 0, 72, 2), A.subtract)
+    ts(W("od"), W("od"), Q(6), A.mult)
+    tt(L("o", EV, 36), L("od", 0, 36), L("oi", 0, 36, 2), A.add)
+    tt(L("o", OD, 36), L("od", 36, 36), L("oi", 72, 36, 2), A.add)
+    ts(W("pt"), W("raw"), -144, A.add, idx=W("cl"))
+    walk()
+    score_lists(0)
+    quant(128, "v", "vt")
+
+    for t in range(3):
+        dst = T.cores[rank ^ STEP[t]]
+        tt(W("ge"), W("sw"), W("diag"), A.mult, idx=W("so"))
+        scan(W("ee"), W("keepf"), W("ge"))
+        n = 12 if t % 2 == 0 else 9
+        for a in range(3):
+            p = (32 * a, 32 * a + 32)
+            ev, od = L("ee", 15 if n == 12 else 63, n, 16, *p), L("ee", 207, n, 16, *p)
+            tt(L("xb", 4 * a, n, 12, *p), *((ev, od) if n == 12 else (od, ev)), A.is_gt)
+        quant(128, "b", "xb")
+        mm(7, 128, "l", 0, "b")
+        m = 3 * n
+        lo, hi = (L("o", EV, 36), L("o", OD, 36)) if n == 12 else (L("o", OD, 27), L("o", EV + 9, 27))
+        tt(L("mm", 0, m), L("ps7", 0, m), L("dd", 0, m), A.mult)
+        tt(lo, lo, L("mm", 0, m), A.add)
+        tt(hi, hi, L("mm", 0, m), A.subtract)
+        for e in range(2):
+            act(L("ab", 81 * e, 81), W("o"), AF.Abs, bias=Q(4 + e))
+        for e in range(2):
+            act(L("oh", 81 * e, 81), L("ab", 81 * e, 81), AF.Relu, bias=1.0, scale=-1.0)
+        walk()
+        for e in range(2):
+            tt(L("pm", e, 81, 2), last(0, BL), L("oh", 81 * e, 81), A.mult)
+        tt(W("p1"), L("pm", 0, 72), L("pm", 90, 72), A.add)
+        tt(W("p2"), L("p1", 0, 36), L("p1", 36, 36), A.add)
+        tt(W("p3"), L("p2", 0, 18), L("p2", 18, 18), A.add)
+        ts(W("uf"), W("p3"), 1296, A.add)
+        copy(W("fg"), W("pt"), idx=W("uf"))
+        turn(W("ft"), W("fg"))
+        al, bl, ll = W("al%d" % t), W("bl%d" % t), W("ll%d" % t)
+        ts(al, L("ft", 0, 18, 16), 144, A.add)
+        send(dst, ll, al, "la%d" % t, "lb%d" % t)
+        ts(W("ub"), L("ft", 0, 18, 16), Q(3), A.add)
+        tt(W("gb"), W("pt"), L("diag", 0, 288), A.mult, idx=W("ub"))
+        scan(W("sb"), L("keepb", 0, 288), W("gb"))
+        ts(bl, L("sb", 15, 18, 16), 144, A.add)
+        for b in range(4):
+            bank = 4 + b if b < 3 else 0
+            mm(bank, 288, "e", 128 * b, "p%d" % t)
+            act(W("d%d" % b), L("ps%d" % bank, 0, 288), AF.Copy)
+        if t < 2:
+            score_lists(t + 1)
+        else:
+            for k in range(8):
+                act(L("ok", 9 * k, 9), L("o", 9 * blk(k), 9), AF.Copy)
+            turn(W("ot"), W("ok"))
+            dmas([("y", T.old[32 * i:32 * i + r, :], T.ot[0:r, 32 * i:32 * i + 32], [L("ot", 32 * i, 32, 1, 0, r)],
+                   [L("old", 0, 32, 1, 32 * i, 32 * i + r)]) for i, r in ((0, 32), (1, 32), (2, 8))])
+            dmas([("y", T.ol[:, :], T.old[:, :], [L("old", 0, 32, 1, 0, 72)], [])])
+        z = "z%d" % t
+        for b in (0, 2, 1, 3):
+            if b < 2:
+                copy(L(z, b, 288, 4), W("d%d" % b), idx=ll)
+            else:
+                act(L(z, b, 288, 4), W("d%d" % b), AF.Copy, idx=ll)
+        quant(288, z, z)
+        for b in range(4):
+            mm(1 + b, 288, "w", 128 * b, z)
+            act(W("r%d" % b), L("ps%d" % (1 + b), 0, 288), AF.Identity, scale=0.03125)
+        for b in range(4):
+            tt(L("x%d" % (t + 1), b, 288, 4), W("r%d" % b), W("f%d" % b), A.add, idx=bl)
+        products(t + 1)
+
+    for h in range(2):
+        mm(5 + h, 144, "v", 0, "x3", 144 * h)
+    copy(L("yt", 0, 144), L("ps5", 0, 144))
+    act(L("yt", 144, 144), L("ps6", 0, 144), AF.Copy)
+    dmas([("y", T.oc[:, :], u8(W("Cx3")), [W("Cx3")], [])]
+         + [("s", T.osc[4 * k:4 * k + 4, :], T.Sx3[32 * k:32 * k + 4, 0:288], [W("Sx3")], []) for k in range(4)])
+    dmas([("y", T.y[:, :], T.yt[:, :], [W("yt")], [])])
+    for sem in sorted(total):
+        if waited.get(sem, 0) < total[sem]:
+            g.sync.wait_ge(T.sem[sem], total[sem])

@@ -1,8 +1,10 @@
+import math
 from concourse.mybir import dt, AluOpType, ActivationFunctionType
 
 STEP = (4, 1, 2)
 NB = 9
 BL = 9
+PARTS = ((0, 4), (4, 5))
 
 
 def blk(k):
@@ -12,13 +14,13 @@ def blk(k):
 BF, F32, I32, U16, F16 = "bfloat16", "float32", "int32", "uint16", "float16"
 SCRATCH = {}
 for _d, _names in (
-        (BF, "diag 384 keepb 384 keepl 288 et 2048 lt 512 ut 512 vt 512 pt 2304 gm 2592 oh 162 fg 288 ft 288 gb 288 sb 288 xb 512 "
+        (BF, "diag 384 keepb 384 keepl 288 et 2048 lt 512 ut 512 vt 512 pt 2304 gm 2880 oh 162 fg 288 ft 288 gb 288 sb 288 xb 512 "
              "f0 288 f1 288 f2 288 f3 288 d0 288 d1 288 d2 288 d3 288 x0 1152 x1 1152 x2 1152 x3 1152 z0 1152 z1 1152 z2 1152"),
         (F32, "pf 8 keepf 384 jm 9 o 81 od 72 dd 36 mm 36 ab 162 dv 72 sov 72 sw 2304 ge 384 ee 384 ok 96 ot 96 yt 288 "
-              "r0 288 r1 288 r2 288 r3 288"),
-        (I32, "pi 8 io 128 ioa 128 ip 384 ipa 384 ie 384 iea 384 ieb 384 ji 9 cli 144 uli 64 raw 2304 oi 144"),
-        (U16, "cl 144 ul 64 uo 90 uf 18 ub 18 so 24 al0 18 al1 18 al2 18 bl0 18 bl1 18 bl2 18 ll0 18 ll1 18 ll2 18"),
-        (F16, "sc 2592 pm 162 p1 72 p2 36 p3 18")):
+              "r0 288 r1 288 r2 288 r3 288 cx 9 cd 9 cv 9"),
+        (I32, "pi 8 io 128 ioa 128 ip 384 ipa 384 ie 384 iea 768 ji 9 cli 72 uli 64 raw 2304 oi 144"),
+        (U16, "cl 72 ul 64 uo 90 uf 18 ub 18 so 24 al0 18 al1 18 al2 18 bl0 18 bl1 18 bl2 18 ll0 18 ll1 18 ll2 18 cu 10"),
+        (F16, "sc 2880 pm 144 pq 126")):
     _w = _names.split()
     for _n, _c in zip(_w[0::2], _w[1::2]):
         SCRATCH[_n] = ("sbuf", [128, int(_c)], _d)
@@ -28,8 +30,10 @@ for _n, _c in (("e", 512), ("l", 128), ("u", 128), ("r", 1024), ("v", 128), ("w"
 SCRATCH["old"] = ("dram", [72, 32], F32)
 for _b in range(8):
     SCRATCH["ps%d" % _b] = ("psum", [128, 512], F32)
-SEMAPHORES = ["vq_", "sq_", "tq_", "gq_"] + ["dm%d" % i for i in range(16)] + [
+SEMAPHORES = ["vq_", "sq_", "tq_", "gq_"] + ["dm%d" % i for i in range(20)] + [
     n + str(t) for t in range(3) for n in ("ca", "cb", "sa", "sb", "la", "lb")]
+ORDER = []
+WAKE, NEAR = 100.0, 40.0
 
 
 def rank_program(g, core, T, topo):
@@ -38,8 +42,7 @@ def rank_program(g, core, T, topo):
         return
     A, AF = AluOpType, ActivationFunctionType
     queue = {"v": g.vector, "s": g.scalar, "t": g.tensor, "g": g, "y": g.sync}
-    known = {e: {} for e in queue}
-    total, waited, snap, recs = {}, {}, {}, {}
+    ops, recs = [], {}
 
     def L(name, lo, n, st=1, p0=0, p1=128):
         return (name, lo, lo + st * (n - 1) + 1, st, p0, p1)
@@ -60,127 +63,116 @@ def rank_program(g, core, T, topo):
             return True
         if a[1] >= b[2] or b[1] >= a[2] or a[4] >= b[5] or b[4] >= a[5]:
             return False
-        return not (a[3] == b[3] and a[3] > 1 and (a[1] - b[1]) % a[3])
+        return (a[1] - b[1]) % math.gcd(a[3], b[3]) == 0
 
-    def need(e, reads, writes, asyn=False):
-        want = {}
+    def rec(q, call, reads, writes, dur, sem, inc=1, lat=0.0, group=None):
+        n, wait = len(ops), set()
         for acc, w in [(r, False) for r in reads] + [(r, True) for r in writes]:
-            for e2, sem, val, w2, acc2 in recs.get(acc[0], []):
-                if not (w or w2 or acc[0].startswith("ps")) or not clash(acc, acc2):
-                    continue
-                if e2 == e and not asyn and not w2:
-                    continue
-                if val > known[e].get(sem, 0):
-                    want[sem] = max(want.get(sem, 0), val)
-        for sem, val in sorted(want.items(), key=lambda kv: -kv[1]):
-            if known[e].get(sem, 0) >= val:
-                continue
-            queue[e].wait_ge(T.sem[sem], val)
-            waited[sem] = max(waited.get(sem, 0), val)
-            known[e][sem] = val
-            for s2, v2 in snap.get((sem, val), {}).items():
-                known[e][s2] = max(known[e].get(s2, 0), v2)
-
-    def note(e2, sem, val, reads, writes):
+            for m, w2, acc2 in recs.get(acc[0], []):
+                bank = acc[0].startswith("ps") and ops[m]["q"] != q
+                if m != n and not (group and ops[m]["group"] == group) and (w or w2 or bank) and clash(acc, acc2):
+                    wait.update(ops[m]["mates"])
         for acc in writes:
-            recs[acc[0]] = [r for r in recs.get(acc[0], []) for b in [r[4]] if not (
+            recs[acc[0]] = [r for r in recs.get(acc[0], []) for b in [r[2]] if not (
                 acc[1] <= b[1] and b[2] <= acc[2] and acc[4] <= b[4] and b[5] <= acc[5]
                 and (acc[3] == 1 or (acc[3] == b[3] and (acc[1] - b[1]) % acc[3] == 0)))]
         for acc, w in [(r, False) for r in reads] + [(r, True) for r in writes]:
-            recs.setdefault(acc[0], []).append((e2, sem, val, w, acc))
+            recs.setdefault(acc[0], []).append((n, w, acc))
+        ops.append(dict(q=q, call=call, dur=dur, lat=lat, wait=wait, sem=sem, inc=inc, group=group, mates=[n]))
+        return n
 
-    def do(e, call, reads, writes):
-        need(e, reads, writes)
-        sem = e + "q_"
-        total[sem] = total.get(sem, 0) + 1
-        call().then_inc(T.sem[sem], 1)
-        snap[(sem, total[sem])] = dict(known[e])
-        note(e, sem, total[sem], reads, writes)
+    def size(v):
+        return (v[2] - v[1] - 1) // v[3] + 1
+
+    def cost(q, out, ins, idx, two=False):
+        n = size(out)
+        if idx:
+            return 60 + 1.4 * size(idx) * 16
+        two_byte = all(SCRATCH[v[0]][2] in (BF, F16, U16) for v in [out] + ins)
+        return 0.9 * max(64, n * (2 if two and not ins[0][0].startswith("ps") else 0.5 if two_byte and q == "v" and not two else 1))
+
+    def do(q, call, reads, writes, dur):
+        rec(q, lambda: call().then_inc(T.sem[q + "q_"], 1), reads, writes, dur, q + "q_")
 
     nd = [0]
 
-    def dmas(jobs):
+    def dmas(jobs, lat=2500.0):
         sem = "dm%d" % nd[0]
         nd[0] += 1
-        total[sem] = 16 * len(jobs)
-        k = {}
-        for e, out, in_, reads, writes in jobs:
-            need(e, reads, writes, True)
-            queue[e].dma_start(out, in_).then_inc(T.sem[sem], 16)
-            for s2, v2 in known[e].items():
-                k[s2] = max(k.get(s2, 0), v2)
-        snap[(sem, total[sem])] = k
-        for e, out, in_, reads, writes in jobs:
-            note("dma", sem, total[sem], reads, writes)
+        ids = [rec(e, lambda e=e, o=o, i=i: queue[e].dma_start(o, i).then_inc(T.sem[sem], 16), rd, wr, 60.0, sem, 16 * len(jobs), lat, sem)
+               for e, o, i, rd, wr in jobs]
+        for i in ids:
+            ops[i]["mates"] = ids
 
-    def send(dst, out, in_, arr, loc, code=False):
-        need("g", [in_], [], True)
+    def send(dst, out, in_, arr, loc, code=False, lat=2500.0):
         rid, pid = topo.addr(dst, core)
         n = len(topo.engines(core, dst))
         f = u8 if code else ap
-        g.remote_dma(f(out), f(in_), T.sem[arr], T.sem[loc], pid, rid, topo.mask(core, dst))
-        total[arr] = total[loc] = n
-        snap[(loc, n)] = dict(known["g"])
-        note("dma", loc, n, [in_], [])
-        note("dma", arr, n, [], [out])
+        s = rec("g", lambda: g.remote_dma(f(out), f(in_), T.sem[arr], T.sem[loc], pid, rid, topo.mask(core, dst)), [in_], [], 100.0, loc, n, lat)
+        r = rec(None, None, [], [out], 0.0, arr, n, lat)
+        ops[r]["wait"].add(s)
 
     def more(*vs):
         return [v for v in vs if isinstance(v, tuple)]
 
     def tt(out, a, b, op, idx=None):
-        do("v", lambda: g.vector.tensor_tensor(ap(out), ap(a, idx), ap(b), op), [a, b] + more(idx), [out])
+        do("v", lambda: g.vector.tensor_tensor(ap(out), ap(a, idx), ap(b), op), [a, b] + more(idx), [out], cost("v", out, [a, b], idx, True))
 
     def ts(out, a, s1, op0, s2=None, op1=None, idx=None):
         c = [ap(s) if isinstance(s, tuple) else s for s in (s1, s2)]
-        ops = (op0,) if op1 is None else (op0, op1)
-        do("v", lambda: g.vector.tensor_scalar(ap(out), ap(a, idx), c[0], c[1], *ops), [a] + more(s1, s2, idx), [out])
+        o2 = (op0,) if op1 is None else (op0, op1)
+        do("v", lambda: g.vector.tensor_scalar(ap(out), ap(a, idx), c[0], c[1], *o2), [a] + more(s1, s2, idx), [out], cost("v", out, [a], idx))
 
     def copy(out, a, idx=None):
-        do("v", lambda: g.vector.tensor_copy(ap(out), ap(a, idx)), [a] + more(idx), [out])
+        do("v", lambda: g.vector.tensor_copy(ap(out), ap(a, idx)), [a] + more(idx), [out], cost("v", out, [a], idx))
 
     def scan(out, d0, d1):
-        do("v", lambda: g.vector.tensor_tensor_scan(ap(out), ap(d0), ap(d1), 0.0, A.mult, A.add), [d0, d1], [out])
+        do("v", lambda: g.vector.tensor_tensor_scan(ap(out), ap(d0), ap(d1), 0.0, A.mult, A.add), [d0, d1], [out], cost("v", out, [d0, d1], None))
 
     def turn(out, a):
-        do("v", lambda: g.vector.transpose(ap(out), ap(a)), [a], [out])
+        do("v", lambda: g.vector.transpose(ap(out), ap(a)), [a], [out], cost("v", out, [a], None))
 
     def act(out, a, func, idx=None, **kw):
         k2 = {k: ap(v) if isinstance(v, tuple) else v for k, v in kw.items()}
-        do("s", lambda: g.scalar.activation(ap(out), ap(a, idx), func, **k2), [a] + more(idx, *kw.values()), [out])
+        do("s", lambda: g.scalar.activation(ap(out), ap(a, idx), func, **k2), [a] + more(idx, *kw.values()), [out], cost("s", out, [a], idx))
 
     def quant(n, name, x):
         q, s, v = L("C" + name, 0, n), L("S" + name, 0, n), L(x, 0, 4 * n)
-        do("v", lambda: g.vector.quantize_mx(ap(q), ap(s), ap(v)), [v], [q, s])
+        do("v", lambda: g.vector.quantize_mx(ap(q), ap(s), ap(v)), [v], [q, s], 12 + n)
 
     def mm(bank, n, w, w0, x, x0=0):
         a, b, c, d = L("C" + w, w0, 128), L("S" + w, w0, 128), L("C" + x, x0, n), L("S" + x, x0, n)
         o = L("ps%d" % bank, 0, n)
-        do("t", lambda: g.tensor.matmul_mx(ap(o), ap(a), ap(b), ap(c), ap(d), True, True), [a, b, c, d], [o])
+        do("t", lambda: g.tensor.matmul_mx(ap(o), ap(a), ap(b), ap(c), ap(d), True, True), [a, b, c, d], [o], 0.6 * (n + 16))
 
     def fill(v, k):
-        do("v", lambda: g.vector.memset(ap(v), k), [], [v])
+        do("v", lambda: g.vector.memset(ap(v), k), [], [v], cost("v", v, [], None))
 
     def iota(v, pattern, base, cm):
-        do("g", lambda: g.iota(ap(v), pattern, base, cm), [], [v])
+        do("g", lambda: g.iota(ap(v), pattern, base, cm), [], [v], 130 + 2 * size(v))
 
     q2 = ("y", "s")
-    dmas([(q2[r % 2], T.raw[r:r + 1, :], T.pg[:, :], [], [L("raw", 0, 2304, 1, r, r + 1)]) for r in range(16)])
+    H = 1152
+    for h in range(2):
+        dmas([(q2[r % 2], T.raw[r:r + 1, H * h:H * h + H], T.pg[64 * h:64 * h + 64, :], [], [L("raw", H * h, H, 1, r, r + 1)])
+              for r in range(16)], 2500.0 + 400 * h)
     dmas([(q2[k % 2], T.oi[0:16, c:c + 18], T.og[16 * k:16 * k + 16, :], [], [L("oi", c, 18, 1, 0, 16)])
-          for k in range(8) for c in [18 * (k // 2 + 4 * (k % 2))]])
-    dmas([("y", T.x0[:, :], T.x[:, :], [], [W("x0")])])
-    dmas([("s", T.ut[:, :], T.u[:, :], [], [W("ut")])])
+          for k in range(8) for c in [18 * (k // 2 + 4 * (k % 2))]], 3300.0)
+    dmas([("y", T.x0[:, :], T.x[:, :], [], [W("x0")])], 4000.0)
+    dmas([("s", T.ut[:, :], T.u[:, :], [], [W("ut")])], 4000.0)
+    for name, lo, n, lat in (("raw", 0, H, 8000.0), ("raw", H, H, 10000.0), ("oi", 0, 144, 5000.0)):
+        dmas([(q2[h % 2], T[name][16 * h:16 * h + 16, lo:lo + n], T[name][0:16, lo:lo + n], [L(name, lo, n, 1, 0, 16)],
+               [L(name, lo, n, 1, 16 * h, 16 * h + 16)]) for h in range(1, 8)], lat)
+    dmas([("y", u8(W("Cw")), T.wc[:, :], [], [W("Cw")]), ("y", T.Sw[:, :], T.ws[:, :], [], [W("Sw")]),
+          ("y", T.vt[:, :], T.v[:, :], [], [W("vt")])], 9000.0)
+
     iota(L("pi", 0, 1), [[0, 1]], 0, 1)
     iota(W("uli"), [[16, 8], [0, 8]], 0, 0)
     iota(W("io"), [[-1, 128]], 128, 1)
     iota(W("ip"), [[-1, 384]], 384, 1)
     iota(W("ie"), [[1, 384]], 0, 0)
     iota(W("ji"), [[32, NB]], -144, 0)
-    iota(W("cli"), [[288, 8], [1, 18]], 0, 0)
-    for name, n in (("raw", 2304), ("oi", 144)):
-        dmas([(q2[h % 2], T[name][16 * h:16 * h + 16, :], T[name][0:16, :], [L(name, 0, n, 1, 0, 16)], [L(name, 0, n, 1, 16 * h, 16 * h + 16)])
-              for h in range(1, 8)])
-    dmas([("y", u8(W("Cw")), T.wc[:, :], [], [W("Cw")]), ("y", T.Sw[:, :], T.ws[:, :], [], [W("Sw")]), ("y", T.vt[:, :], T.v[:, :], [], [W("vt")])])
-
+    iota(W("cli"), [[288, 4], [1, 18]], 0, 0)
     copy(W("ul"), W("uli"))
     fill(W("et"), 0.0)
     fill(W("lt"), 0.0)
@@ -192,11 +184,11 @@ def rank_program(g, core, T, topo):
     quant(128, "l", "lt")
     ts(W("ipa"), W("ip"), 15, A.bitwise_and)
     ts(W("diag"), W("ipa"), 0, A.is_equal)
-    ts(W("iea"), W("ie"), 15, A.bitwise_and)
-    ts(W("ieb"), W("ie"), 31, A.bitwise_and)
-    ts(W("keepf"), W("iea"), 0, A.is_gt)
-    ts(W("keepb"), W("iea"), 0, A.is_gt)
-    ts(W("keepl"), L("ieb", 0, 288), 0, A.is_gt)
+    ts(L("iea", 0, 384), W("ie"), 15, A.bitwise_and)
+    ts(L("iea", 384, 384), W("ie"), 31, A.bitwise_and)
+    ts(W("keepf"), L("iea", 0, 384), 0, A.is_gt)
+    ts(W("keepb"), L("iea", 0, 384), 0, A.is_gt)
+    ts(W("keepl"), L("iea", 384, 288), 0, A.is_gt)
     P = lambda j: L("pi", j, 1)
     Q = lambda j: L("pf", j, 1)
     ts(P(1), P(0), 15, A.bitwise_and)
@@ -218,38 +210,45 @@ def rank_program(g, core, T, topo):
     fill(L("o", 36, 9), 8.0)
     quant(128, "u", "ut")
     do("v", lambda: g.vector.tensor_copy(ap(W("Cr")).bitcast(dt.uint32), ap(W("Cu")).bitcast(dt.uint32).indirect(ap(W("ul")))),
-       [W("Cu"), W("ul")], [W("Cr")])
+       [W("Cu"), W("ul")], [W("Cr")], 1500.0)
     act(W("Sr"), W("Su"), AF.Copy, idx=W("ul"))
 
     EV, OD = 0, 45
     base = lambda b0, n: L("gm", 288 * b0 + 1, NB * n, 32)
-    last = lambda b0, n: L("sc", 288 * b0 + 31, NB * n, 32)
-    off = lambda k: L("uo", 10 * k, NB)
+    last = lambda b0, n, b1=0: L("sc", 288 * b0 + 32 * b1 + 31, n, 32)
 
-    def step(k):
-        s = blk(k)
-        tt(L("gm", 288 * s, 144, 2), W("pt"), L("diag", 0, 144), A.mult, idx=off(k - 1))
-        scan(L("sc", 288 * s, 288), W("keepl"), L("gm", 288 * s, 288))
+    def look(s, name, lo):
+        for b, n in PARTS:
+            c = 288 * s + 32 * b
+            tt(L("gm", c, 16 * n, 2), W("pt"), L("diag", 0, 16 * n), A.mult, idx=L(name, lo + b, n))
+            scan(L("sc", c, 32 * n), L("keepl", 0, 32 * n), L("gm", c, 32 * n))
 
-    def walk():
-        ts(base(0, BL), W("o"), 288, A.mult, -1152, A.add)
-        tt(last(0, 1), base(0, 1), W("jm"), A.add)
-        ts(off(0), last(0, 1), 1296, A.add)
-        for k in range(1, 8):
-            step(k)
-            ts(off(k), last(blk(k), 1), 1296, A.add)
+    def lists(k):
+        for b, n in PARTS:
+            ts(L("uo", 10 * k + b, n), last(blk(k), n, b), 1296, A.add)
+
+    def walk(k0):
+        for k in range(k0 + 1, 8):
+            look(blk(k), "uo", 10 * (k - 1))
+            lists(k)
 
     def score_lists(t):
-        step(8)
-        tt(W("dv"), last(1, 8), base(1, 8), A.subtract)
+        look(4, "uo", 70)
+        tt(W("dv"), last(1, 72), base(1, 8), A.subtract)
         tt(L("sov", 0, 36), L("dv", 36, 36), base(0, 4), A.add)
         tt(L("sov", 36, 36), L("dv", 0, 36), base(5, 4), A.add)
         for a, (p0, p1) in enumerate(((0, 32), (32, 64), (64, 128))):
             ts(L("so", 0, 24, 1, p0, p1), L("sov", a, 24, 3, p0, p1), 1296, A.add)
         if t % 2 == 0:
             tt(L("dd", 0, 36), L("o", OD, 36), L("o", EV, 36), A.subtract)
+            tt(W("cv"), base(5, 1), W("jm"), A.add)
         else:
             tt(L("dd", 0, 27), L("o", EV + 9, 27), L("o", OD, 27), A.subtract)
+            tt(W("cv"), base(1, 1), L("dv", 36, 9), A.add)
+        ts(L("cu", 0, 9), W("cv"), 1296, A.add)
+        ts(base(9, 1), L("o", EV if t % 2 == 0 else OD, 9), 288, A.mult, -1152, A.add)
+        look(9, "cu", 0)
+        tt(W("cd"), last(9, 9), last(blk(1 + t % 2), 9), A.subtract)
 
     def products(t):
         x = "x%d" % t
@@ -257,8 +256,8 @@ def rank_program(g, core, T, topo):
         if t == 3:
             return
         dst = T.cores[rank ^ STEP[t]]
-        send(dst, W("Cp%d" % t), W("C" + x), "ca%d" % t, "cb%d" % t, True)
-        send(dst, W("Sp%d" % t), W("S" + x), "sa%d" % t, "sb%d" % t)
+        send(dst, W("Cp%d" % t), W("C" + x), "ca%d" % t, "cb%d" % t, True, 6000.0)
+        send(dst, W("Sp%d" % t), W("S" + x), "sa%d" % t, "sb%d" % t, False, 6000.0)
         for i in range(8):
             mm(i, 288, "r", 128 * i, x)
             if i % 2 == 0:
@@ -274,15 +273,20 @@ def rank_program(g, core, T, topo):
     ts(W("od"), W("od"), Q(6), A.mult)
     tt(L("o", EV, 36), L("od", 0, 36), L("oi", 0, 36, 2), A.add)
     tt(L("o", OD, 36), L("od", 36, 36), L("oi", 72, 36, 2), A.add)
-    ts(W("pt"), W("raw"), -144, A.add, idx=W("cl"))
-    walk()
+    ts(base(0, BL), W("o"), 288, A.mult, -1152, A.add)
+    for h in range(2):
+        ts(L("pt", H * h, H), L("raw", H * h, H), -144, A.add, idx=W("cl"))
+    tt(last(0, 9), base(0, 1), W("jm"), A.add)
+    lists(0)
+    walk(0)
     score_lists(0)
     quant(128, "v", "vt")
 
     for t in range(3):
         dst = T.cores[rank ^ STEP[t]]
-        tt(W("ge"), W("sw"), W("diag"), A.mult, idx=W("so"))
-        scan(W("ee"), W("keepf"), W("ge"))
+        for h in (0, 192):
+            tt(L("ge", h, 192), W("sw"), L("diag", 0, 192), A.mult, idx=L("so", h // 16, 12))
+            scan(L("ee", h, 192), L("keepf", 0, 192), L("ge", h, 192))
         n = 12 if t % 2 == 0 else 9
         for a in range(3):
             p = (32 * a, 32 * a + 32)
@@ -290,27 +294,42 @@ def rank_program(g, core, T, topo):
             tt(L("xb", 4 * a, n, 12, *p), *((ev, od) if n == 12 else (od, ev)), A.is_gt)
         quant(128, "b", "xb")
         mm(7, 128, "l", 0, "b")
+        k1 = 1 + t % 2
+        tt(W("cx"), L("ps7", 0, 9), W("cd"), A.mult)
+        tt(last(blk(k1), 9), last(blk(k1), 9), W("cx"), A.add)
+        lists(k1)
         m = 3 * n
         lo, hi = (L("o", EV, 36), L("o", OD, 36)) if n == 12 else (L("o", OD, 27), L("o", EV + 9, 27))
         tt(L("mm", 0, m), L("ps7", 0, m), L("dd", 0, m), A.mult)
         tt(lo, lo, L("mm", 0, m), A.add)
         tt(hi, hi, L("mm", 0, m), A.subtract)
+        ts(base(0, 4), L("o", EV, 36), 288, A.mult, -1152, A.add)
+        ts(base(5, 4), L("o", OD, 36), 288, A.mult, -1152, A.add)
+        if n == 12:
+            tt(last(0, 9), base(0, 1), W("jm"), A.add)
+        else:
+            tt(last(5, 9), base(5, 1), L("dv", 36, 9), A.add)
         for e in range(2):
             act(L("ab", 81 * e, 81), W("o"), AF.Abs, bias=Q(4 + e))
         for e in range(2):
             act(L("oh", 81 * e, 81), L("ab", 81 * e, 81), AF.Relu, bias=1.0, scale=-1.0)
-        walk()
-        for e in range(2):
-            tt(L("pm", e, 81, 2), last(0, BL), L("oh", 81 * e, 81), A.mult)
-        tt(W("p1"), L("pm", 0, 72), L("pm", 90, 72), A.add)
-        tt(W("p2"), L("p1", 0, 36), L("p1", 36, 36), A.add)
-        tt(W("p3"), L("p2", 0, 18), L("p2", 18, 18), A.add)
-        ts(W("uf"), W("p3"), 1296, A.add)
-        copy(W("fg"), W("pt"), idx=W("uf"))
-        turn(W("ft"), W("fg"))
-        al, bl, ll = W("al%d" % t), W("bl%d" % t), W("ll%d" % t)
-        ts(al, L("ft", 0, 18, 16), 144, A.add)
-        send(dst, ll, al, "la%d" % t, "lb%d" % t)
+        walk(k1)
+        for to, b0, nb in ((0, 0, 3), (54, 5, 3), (108, 3, 1), (126, 8, 1)):
+            for e in range(2):
+                tt(L("pm", to + e, NB * nb, 2), last(b0, NB * nb), L("oh", 81 * e + 9 * b0, NB * nb), A.mult)
+        tt(L("pq", 0, 54), L("pm", 0, 54), L("pm", 54, 54), A.add)
+        tt(L("pq", 54, 18), L("pq", 0, 18), L("pq", 18, 18), A.add)
+        tt(L("pq", 72, 18), L("pq", 54, 18), L("pq", 36, 18), A.add)
+        tt(L("pq", 90, 18), L("pq", 72, 18), L("pm", 108, 18), A.add)
+        tt(L("pq", 108, 18), L("pq", 90, 18), L("pm", 126, 18), A.add)
+        ts(W("uf"), L("pq", 108, 18), 1296, A.add)
+        al, bl, ll = "al%d" % t, W("bl%d" % t), W("ll%d" % t)
+        for b, n in PARTS:
+            c = L("fg", 32 * b, 32 * n), L("ft", 32 * b, 32 * n)
+            copy(c[0], W("pt"), idx=L("uf", 2 * b, 2 * n))
+            turn(c[1], c[0])
+            ts(L(al, 2 * b, 2 * n), L("ft", 32 * b, 2 * n, 16), 144, A.add)
+        send(dst, ll, W(al), "la%d" % t, "lb%d" % t)
         ts(W("ub"), L("ft", 0, 18, 16), Q(3), A.add)
         tt(W("gb"), W("pt"), L("diag", 0, 288), A.mult, idx=W("ub"))
         scan(W("sb"), L("keepb", 0, 288), W("gb"))
@@ -346,9 +365,62 @@ def rank_program(g, core, T, topo):
         mm(5 + h, 144, "v", 0, "x3", 144 * h)
     copy(L("yt", 0, 144), L("ps5", 0, 144))
     act(L("yt", 144, 144), L("ps6", 0, 144), AF.Copy)
+    dmas([("y", T.y[:, :], T.yt[:, :], [W("yt")], [])])
     dmas([("y", T.oc[:, :], u8(W("Cx3")), [W("Cx3")], [])]
          + [("s", T.osc[4 * k:4 * k + 4, :], T.Sx3[32 * k:32 * k + 4, 0:288], [W("Sx3")], []) for k in range(4)])
-    dmas([("y", T.y[:, :], T.yt[:, :], [W("yt")], [])])
+
+    if not ORDER:
+        N = len(ops)
+        nxt, left, prio = [[] for _ in ops], [len(o["wait"]) for o in ops], [0.0] * N
+        for i, o in enumerate(ops):
+            for m in o["wait"]:
+                nxt[m].append(i)
+        span = lambda o: (o["lat"] if o["q"] else 0.0) or o["dur"]
+        for i in reversed(range(N)):
+            prio[i] = span(ops[i]) + max([0.0] + [WAKE + prio[k] for k in nxt[i]])
+        ready, free, done = {i: 0.0 for i in range(N) if not left[i]}, {q: 0.0 for q in list(queue) + [None]}, [0.0] * N
+        while ready:
+            begin = {i: max(r, free[ops[i]["q"]]) for i, r in ready.items()}
+            first = min(begin, key=lambda i: (begin[i], -prio[i]))
+            i = max((k for k in begin if ops[k]["q"] == ops[first]["q"] and begin[k] <= begin[first] + NEAR), key=lambda k: (prio[k], -k))
+            o = ops[i]
+            at = ready.pop(i)
+            if o["q"]:
+                free[o["q"]] = begin[i] + o["dur"]
+                done[i] = begin[i] + span(o)
+            else:
+                done[i] = at
+            ORDER.append(i)
+            for k in nxt[i]:
+                left[k] -= 1
+                if not left[k]:
+                    ready[k] = WAKE + max(done[m] for m in ops[k]["wait"])
+
+    known, total, waited, snap, token = {q: {} for q in queue}, {}, {}, {}, {}
+    for i in ORDER:
+        o = ops[i]
+        q, sem = o["q"], o["sem"]
+        if q is None:
+            total[sem], token[i] = o["inc"], (sem, o["inc"])
+            continue
+        want = {}
+        for m in o["wait"]:
+            s, v = token[m]
+            want[s] = max(want.get(s, 0), v)
+        for s, v in sorted(want.items(), key=lambda kv: -kv[1]):
+            if known[q].get(s, 0) >= v:
+                continue
+            queue[q].wait_ge(T.sem[s], v)
+            waited[s] = max(waited.get(s, 0), v)
+            known[q][s] = v
+            for s2, v2 in snap.get((s, v), {}).items():
+                known[q][s2] = max(known[q].get(s2, 0), v2)
+        o["call"]()
+        total[sem] = total.get(sem, 0) + 1 if not o["lat"] else o["inc"]
+        token[i] = (sem, total[sem])
+        seen = snap.setdefault(token[i], {})
+        for s2, v2 in known[q].items():
+            seen[s2] = max(seen.get(s2, 0), v2)
     for sem in sorted(total):
         if waited.get(sem, 0) < total[sem]:
             g.sync.wait_ge(T.sem[sem], total[sem])

import math
from concourse.mybir import dt, AluOpType, ActivationFunctionType

STEP = (4, 1, 2)
NB = 9
BL = 9
PARTS = ((0, 4), (4, 5))


def blk(k):
    return k // 2 if k % 2 == 0 else 5 + k // 2


BF, F32, I32, U16, F16 = "bfloat16", "float32", "int32", "uint16", "float16"
SCRATCH = {}
for _d, _names in (
        (BF, "diag 384 keepb 384 keepl 288 et 2048 lt 512 ut 512 vt 512 pt 2304 gm 2880 oh 162 fg 288 ft 288 gb 288 sb 288 xb 512 "
             "f0 288 f1 288 f2 288 f3 288 d0 288 d1 288 d2 288 d3 288 x0 1152 x1 1152 x2 1152 x3 1152 z0 1152 z1 1152 z2 1152"),
        (F32, "pf 8 keepf 384 jm 9 o 81 od 72 dd 36 mm 36 ab 162 dv 72 sov 72 sw 2304 ge 384 ee 384 ok 96 ot 96 yt 288 "
              "r0 288 r1 288 r2 288 r3 288 cx 9 cd 9 cv 9"),
        (I32, "pi 8 io 128 ioa 128 ip 384 ipa 384 ie 384 iea 768 ji 9 cli 72 uli 64 raw 2304 oi 144"),
        (U16, "cl 72 ul 64 uo 90 uf 18 ub 18 so 24 al0 18 al1 18 al2 18 bl0 18 bl1 18 bl2 18 ll0 18 ll1 18 ll2 18 cu 10"),
        (F16, "sc 2880 pm 144 pq 126")):
    _w = _names.split()
    for _n, _c in zip(_w[0::2], _w[1::2]):
        SCRATCH[_n] = ("sbuf", [128, int(_c)], _d)
for _n, _c in (("e", 512), ("l", 128), ("u", 128), ("r", 1024), ("v", 128), ("w", 512), ("b", 128)) + tuple(
        (_m, 288) for _m in ("x0", "x1", "x2", "x3", "p0", "p1", "p2", "z0", "z1", "z2")):
    SCRATCH["C" + _n], SCRATCH["S" + _n] = ("sbuf", [128, _c], "float8_e4m3fn_x4"), ("sbuf", [128, _c], "uint8")
SCRATCH["old"] = ("dram", [72, 32], F32)
for _b in range(8):
    SCRATCH["ps%d" % _b] = ("psum", [128, 512], F32)
SEMAPHORES = ["vq_", "sq_", "tq_", "gq_"] + ["dm%d" % i for i in range(20)] + [
    n + str(t) for t in range(3) for n in ("ca", "cb", "sa", "sb", "la", "lb")]
ORDER = []
WAKE, NEAR = 100.0, 40.0


def rank_program(g, core, T, topo):
    rank = T.rank_of(core)
    if rank is None:
        return
    A, AF = AluOpType, ActivationFunctionType
    queue = {"v": g.vector, "s": g.scalar, "t": g.tensor, "g": g, "y": g.sync}
    ops, recs = [], {}

    def L(name, lo, n, st=1, p0=0, p1=128):
        return (name, lo, lo + st * (n - 1) + 1, st, p0, p1)

    def W(name):
        return (name, 0, SCRATCH[name][1][1], 1, 0, 128)

    def ap(v, idx=None):
        name, lo, hi, st, p0, p1 = v
        a = T[name][p0:p1, lo:hi] if st == 1 else T[name][p0:p1, lo:hi:st]
        return a.indirect(ap(idx)) if idx else a

    def u8(v):
        return ap(v).bitcast(dt.uint8)

    def clash(a, b):
        if a[0].startswith("ps"):
            return True
        if a[1] >= b[2] or b[1] >= a[2] or a[4] >= b[5] or b[4] >= a[5]:
            return False
        return (a[1] - b[1]) % math.gcd(a[3], b[3]) == 0

    def rec(q, call, reads, writes, dur, sem, inc=1, lat=0.0, group=None):
        n, wait = len(ops), set()
        for acc, w in [(r, False) for r in reads] + [(r, True) for r in writes]:
            for m, w2, acc2 in recs.get(acc[0], []):
                bank = acc[0].startswith("ps") and ops[m]["q"] != q
                if m != n and not (group and ops[m]["group"] == group) and (w or w2 or bank) and clash(acc, acc2):
                    wait.update(ops[m]["mates"])
        for acc in writes:
            recs[acc[0]] = [r for r in recs.get(acc[0], []) for b in [r[2]] if not (
                acc[1] <= b[1] and b[2] <= acc[2] and acc[4] <= b[4] and b[5] <= acc[5]
                and (acc[3] == 1 or (acc[3] == b[3] and (acc[1] - b[1]) % acc[3] == 0)))]
        for acc, w in [(r, False) for r in reads] + [(r, True) for r in writes]:
            recs.setdefault(acc[0], []).append((n, w, acc))
        ops.append(dict(q=q, call=call, dur=dur, lat=lat, wait=wait, sem=sem, inc=inc, group=group, mates=[n]))
        return n

    def size(v):
        return (v[2] - v[1] - 1) // v[3] + 1

    def cost(q, out, ins, idx, two=False):
        n = size(out)
        if idx:
            return 60 + 1.4 * size(idx) * 16
        two_byte = all(SCRATCH[v[0]][2] in (BF, F16, U16) for v in [out] + ins)
        return 0.9 * max(64, n * (2 if two and not ins[0][0].startswith("ps") else 0.5 if two_byte and q == "v" and not two else 1))

    def do(q, call, reads, writes, dur):
        rec(q, lambda: call().then_inc(T.sem[q + "q_"], 1), reads, writes, dur, q + "q_")

    nd = [0]

    def dmas(jobs, lat=2500.0):
        sem = "dm%d" % nd[0]
        nd[0] += 1
        ids = [rec(e, lambda e=e, o=o, i=i: queue[e].dma_start(o, i).then_inc(T.sem[sem], 16), rd, wr, 60.0, sem, 16 * len(jobs), lat, sem)
               for e, o, i, rd, wr in jobs]
        for i in ids:
            ops[i]["mates"] = ids

    def send(dst, out, in_, arr, loc, code=False, lat=2500.0):
        rid, pid = topo.addr(dst, core)
        n = len(topo.engines(core, dst))
        f = u8 if code else ap
        s = rec("g", lambda: g.remote_dma(f(out), f(in_), T.sem[arr], T.sem[loc], pid, rid, topo.mask(core, dst)), [in_], [], 100.0, loc, n, lat)
        r = rec(None, None, [], [out], 0.0, arr, n, lat)
        ops[r]["wait"].add(s)

    def more(*vs):
        return [v for v in vs if isinstance(v, tuple)]

    def tt(out, a, b, op, idx=None):
        do("v", lambda: g.vector.tensor_tensor(ap(out), ap(a, idx), ap(b), op), [a, b] + more(idx), [out], cost("v", out, [a, b], idx, True))

    def ts(out, a, s1, op0, s2=None, op1=None, idx=None):
        c = [ap(s) if isinstance(s, tuple) else s for s in (s1, s2)]
        o2 = (op0,) if op1 is None else (op0, op1)
        do("v", lambda: g.vector.tensor_scalar(ap(out), ap(a, idx), c[0], c[1], *o2), [a] + more(s1, s2, idx), [out], cost("v", out, [a], idx))

    def copy(out, a, idx=None):
        do("v", lambda: g.vector.tensor_copy(ap(out), ap(a, idx)), [a] + more(idx), [out], cost("v", out, [a], idx))

    def scan(out, d0, d1):
        do("v", lambda: g.vector.tensor_tensor_scan(ap(out), ap(d0), ap(d1), 0.0, A.mult, A.add), [d0, d1], [out], cost("v", out, [d0, d1], None))

    def turn(out, a):
        do("v", lambda: g.vector.transpose(ap(out), ap(a)), [a], [out], cost("v", out, [a], None))

    def act(out, a, func, idx=None, **kw):
        k2 = {k: ap(v) if isinstance(v, tuple) else v for k, v in kw.items()}
        do("s", lambda: g.scalar.activation(ap(out), ap(a, idx), func, **k2), [a] + more(idx, *kw.values()), [out], cost("s", out, [a], idx))

    def quant(n, name, x):
        q, s, v = L("C" + name, 0, n), L("S" + name, 0, n), L(x, 0, 4 * n)
        do("v", lambda: g.vector.quantize_mx(ap(q), ap(s), ap(v)), [v], [q, s], 12 + n)

    def mm(bank, n, w, w0, x, x0=0):
        a, b, c, d = L("C" + w, w0, 128), L("S" + w, w0, 128), L("C" + x, x0, n), L("S" + x, x0, n)
        o = L("ps%d" % bank, 0, n)
        do("t", lambda: g.tensor.matmul_mx(ap(o), ap(a), ap(b), ap(c), ap(d), True, True), [a, b, c, d], [o], 0.6 * (n + 16))

    def fill(v, k):
        do("v", lambda: g.vector.memset(ap(v), k), [], [v], cost("v", v, [], None))

    def iota(v, pattern, base, cm):
        do("g", lambda: g.iota(ap(v), pattern, base, cm), [], [v], 130 + 2 * size(v))

    q2 = ("y", "s")
    H = 1152
    for h in range(2):
        dmas([(q2[r % 2], T.raw[r:r + 1, H * h:H * h + H], T.pg[64 * h:64 * h + 64, :], [], [L("raw", H * h, H, 1, r, r + 1)])
              for r in range(16)], 2500.0 + 400 * h)
    dmas([(q2[k % 2], T.oi[0:16, c:c + 18], T.og[16 * k:16 * k + 16, :], [], [L("oi", c, 18, 1, 0, 16)])
          for k in range(8) for c in [18 * (k // 2 + 4 * (k % 2))]], 3300.0)
    dmas([("y", T.x0[:, :], T.x[:, :], [], [W("x0")])], 4000.0)
    dmas([("s", T.ut[:, :], T.u[:, :], [], [W("ut")])], 4000.0)
    for name, lo, n, lat in (("raw", 0, H, 8000.0), ("raw", H, H, 10000.0), ("oi", 0, 144, 5000.0)):
        dmas([(q2[h % 2], T[name][16 * h:16 * h + 16, lo:lo + n], T[name][0:16, lo:lo + n], [L(name, lo, n, 1, 0, 16)],
               [L(name, lo, n, 1, 16 * h, 16 * h + 16)]) for h in range(1, 8)], lat)
    dmas([("y", u8(W("Cw")), T.wc[:, :], [], [W("Cw")]), ("y", T.Sw[:, :], T.ws[:, :], [], [W("Sw")]),
          ("y", T.vt[:, :], T.v[:, :], [], [W("vt")])], 9000.0)

    iota(L("pi", 0, 1), [[0, 1]], 0, 1)
    iota(W("uli"), [[16, 8], [0, 8]], 0, 0)
    iota(W("io"), [[-1, 128]], 128, 1)
    iota(W("ip"), [[-1, 384]], 384, 1)
    iota(W("ie"), [[1, 384]], 0, 0)
    iota(W("ji"), [[32, NB]], -144, 0)
    iota(W("cli"), [[288, 4], [1, 18]], 0, 0)
    copy(W("ul"), W("uli"))
    fill(W("et"), 0.0)
    fill(W("lt"), 0.0)
    for b in range(4):
        ts(L("et", 512 * b + b, 128, 4), W("io"), 128, A.is_equal)
    ts(W("ioa"), W("io"), 31, A.bitwise_and)
    ts(L("lt", 0, 128, 4), W("ioa"), 0, A.is_equal)
    quant(512, "e", "et")
    quant(128, "l", "lt")
    ts(W("ipa"), W("ip"), 15, A.bitwise_and)
    ts(W("diag"), W("ipa"), 0, A.is_equal)
    ts(L("iea", 0, 384), W("ie"), 15, A.bitwise_and)
    ts(L("iea", 384, 384), W("ie"), 31, A.bitwise_and)
    ts(W("keepf"), L("iea", 0, 384), 0, A.is_gt)
    ts(W("keepb"), L("iea", 0, 384), 0, A.is_gt)
    ts(W("keepl"), L("iea", 384, 288), 0, A.is_gt)
    P = lambda j: L("pi", j, 1)
    Q = lambda j: L("pf", j, 1)
    ts(P(1), P(0), 15, A.bitwise_and)
    ts(P(2), P(0), 31, A.bitwise_and)
    ts(P(3), P(0), 4, A.arith_shift_right)
    ts(P(4), P(0), 5, A.arith_shift_right)
    ts(P(5), P(3), 1, A.bitwise_and)
    ts(Q(1), P(1), 18, A.mult)
    ts(Q(2), P(2), 0, A.add)
    ts(Q(3), P(3), 288, A.mult, 144, A.add)
    ts(Q(4), P(4), -2, A.mult)
    ts(Q(5), P(4), -2, A.mult, -1, A.add)
    ts(Q(6), P(5), 0, A.add)
    ts(W("jm"), W("ji"), Q(2), A.add)
    ts(W("cl"), W("cli"), Q(1), A.add)
    fill(W("gm"), 0.0)
    fill(W("xb"), 0.0)
    fill(L("ok", 72, 24), 0.0)
    fill(L("o", 36, 9), 8.0)
    quant(128, "u", "ut")
    do("v", lambda: g.vector.tensor_copy(ap(W("Cr")).bitcast(dt.uint32), ap(W("Cu")).bitcast(dt.uint32).indirect(ap(W("ul")))),
       [W("Cu"), W("ul")], [W("Cr")], 1500.0)
    act(W("Sr"), W("Su"), AF.Copy, idx=W("ul"))

    EV, OD = 0, 45
    base = lambda b0, n: L("gm", 288 * b0 + 1, NB * n, 32)
    last = lambda b0, n, b1=0: L("sc", 288 * b0 + 32 * b1 + 31, n, 32)

    def look(s, name, lo):
        for b, n in PARTS:
            c = 288 * s + 32 * b
            tt(L("gm", c, 16 * n, 2), W("pt"), L("diag", 0, 16 * n), A.mult, idx=L(name, lo + b, n))
            scan(L("sc", c, 32 * n), L("keepl", 0, 32 * n), L("gm", c, 32 * n))

    def lists(k):
        for b, n in PARTS:
            ts(L("uo", 10 * k + b, n), last(blk(k), n, b), 1296, A.add)

    def walk(k0):
        for k in range(k0 + 1, 8):
            look(blk(k), "uo", 10 * (k - 1))
            lists(k)

    def score_lists(t):
        look(4, "uo", 70)
        tt(W("dv"), last(1, 72), base(1, 8), A.subtract)
        tt(L("sov", 0, 36), L("dv", 36, 36), base(0, 4), A.add)
        tt(L("sov", 36, 36), L("dv", 0, 36), base(5, 4), A.add)
        for a, (p0, p1) in enumerate(((0, 32), (32, 64), (64, 128))):
            ts(L("so", 0, 24, 1, p0, p1), L("sov", a, 24, 3, p0, p1), 1296, A.add)
        if t % 2 == 0:
            tt(L("dd", 0, 36), L("o", OD, 36), L("o", EV, 36), A.subtract)
            tt(W("cv"), base(5, 1), W("jm"), A.add)
        else:
            tt(L("dd", 0, 27), L("o", EV + 9, 27), L("o", OD, 27), A.subtract)
            tt(W("cv"), base(1, 1), L("dv", 36, 9), A.add)
        ts(L("cu", 0, 9), W("cv"), 1296, A.add)
        ts(base(9, 1), L("o", EV if t % 2 == 0 else OD, 9), 288, A.mult, -1152, A.add)
        look(9, "cu", 0)
        tt(W("cd"), last(9, 9), last(blk(1 + t % 2), 9), A.subtract)

    def products(t):
        x = "x%d" % t
        quant(288, x, x)
        if t == 3:
            return
        dst = T.cores[rank ^ STEP[t]]
        send(dst, W("Cp%d" % t), W("C" + x), "ca%d" % t, "cb%d" % t, True, 6000.0)
        send(dst, W("Sp%d" % t), W("S" + x), "sa%d" % t, "sb%d" % t, False, 6000.0)
        for i in range(8):
            mm(i, 288, "r", 128 * i, x)
            if i % 2 == 0:
                copy(L("sw", 288 * i, 288), L("ps%d" % i, 0, 288))
            else:
                act(L("sw", 288 * i, 288), L("ps%d" % i, 0, 288), AF.Copy)
        for b in range(4):
            mm(b, 288, "e", 128 * b, x)
            act(W("f%d" % b), L("ps%d" % b, 0, 288), AF.Copy)

    products(0)
    tt(W("od"), L("oi", 1, 72, 2), L("oi", 0, 72, 2), A.subtract)
    ts(W("od"), W("od"), Q(6), A.mult)
    tt(L("o", EV, 36), L("od", 0, 36), L("oi", 0, 36, 2), A.add)
    tt(L("o", OD, 36), L("od", 36, 36), L("oi", 72, 36, 2), A.add)
    ts(base(0, BL), W("o"), 288, A.mult, -1152, A.add)
    for h in range(2):
        ts(L("pt", H * h, H), L("raw", H * h, H), -144, A.add, idx=W("cl"))
    tt(last(0, 9), base(0, 1), W("jm"), A.add)
    lists(0)
    walk(0)
    score_lists(0)
    quant(128, "v", "vt")

    for t in range(3):
        dst = T.cores[rank ^ STEP[t]]
        for h in (0, 192):
            tt(L("ge", h, 192), W("sw"), L("diag", 0, 192), A.mult, idx=L("so", h // 16, 12))
            scan(L("ee", h, 192), L("keepf", 0, 192), L("ge", h, 192))
        n = 12 if t % 2 == 0 else 9
        for a in range(3):
            p = (32 * a, 32 * a + 32)
            ev, od = L("ee", 15 if n == 12 else 63, n, 16, *p), L("ee", 207, n, 16, *p)
            tt(L("xb", 4 * a, n, 12, *p), *((ev, od) if n == 12 else (od, ev)), A.is_gt)
        quant(128, "b", "xb")
        mm(7, 128, "l", 0, "b")
        k1 = 1 + t % 2
        tt(W("cx"), L("ps7", 0, 9), W("cd"), A.mult)
        tt(last(blk(k1), 9), last(blk(k1), 9), W("cx"), A.add)
        lists(k1)
        m = 3 * n
        lo, hi = (L("o", EV, 36), L("o", OD, 36)) if n == 12 else (L("o", OD, 27), L("o", EV + 9, 27))
        tt(L("mm", 0, m), L("ps7", 0, m), L("dd", 0, m), A.mult)
        tt(lo, lo, L("mm", 0, m), A.add)
        tt(hi, hi, L("mm", 0, m), A.subtract)
        ts(base(0, 4), L("o", EV, 36), 288, A.mult, -1152, A.add)
        ts(base(5, 4), L("o", OD, 36), 288, A.mult, -1152, A.add)
        if n == 12:
            tt(last(0, 9), base(0, 1), W("jm"), A.add)
        else:
            tt(last(5, 9), base(5, 1), L("dv", 36, 9), A.add)
        for e in range(2):
            act(L("ab", 81 * e, 81), W("o"), AF.Abs, bias=Q(4 + e))
        for e in range(2):
            act(L("oh", 81 * e, 81), L("ab", 81 * e, 81), AF.Relu, bias=1.0, scale=-1.0)
        walk(k1)
        for to, b0, nb in ((0, 0, 3), (54, 5, 3), (108, 3, 1), (126, 8, 1)):
            for e in range(2):
                tt(L("pm", to + e, NB * nb, 2), last(b0, NB * nb), L("oh", 81 * e + 9 * b0, NB * nb), A.mult)
        tt(L("pq", 0, 54), L("pm", 0, 54), L("pm", 54, 54), A.add)
        tt(L("pq", 54, 18), L("pq", 0, 18), L("pq", 18, 18), A.add)
        tt(L("pq", 72, 18), L("pq", 54, 18), L("pq", 36, 18), A.add)
        tt(L("pq", 90, 18), L("pq", 72, 18), L("pm", 108, 18), A.add)
        tt(L("pq", 108, 18), L("pq", 90, 18), L("pm", 126, 18), A.add)
        ts(W("uf"), L("pq", 108, 18), 1296, A.add)
        al, bl, ll = "al%d" % t, W("bl%d" % t), W("ll%d" % t)
        for b, n in PARTS:
            c = L("fg", 32 * b, 32 * n), L("ft", 32 * b, 32 * n)
            copy(c[0], W("pt"), idx=L("uf", 2 * b, 2 * n))
            turn(c[1], c[0])
            ts(L(al, 2 * b, 2 * n), L("ft", 32 * b, 2 * n, 16), 144, A.add)
        send(dst, ll, W(al), "la%d" % t, "lb%d" % t)
        ts(W("ub"), L("ft", 0, 18, 16), Q(3), A.add)
        tt(W("gb"), W("pt"), L("diag", 0, 288), A.mult, idx=W("ub"))
        scan(W("sb"), L("keepb", 0, 288), W("gb"))
        ts(bl, L("sb", 15, 18, 16), 144, A.add)
        for b in range(4):
            bank = 4 + b if b < 3 else 0
            mm(bank, 288, "e", 128 * b, "p%d" % t)
            act(W("d%d" % b), L("ps%d" % bank, 0, 288), AF.Copy)
        if t < 2:
            score_lists(t + 1)
        else:
            for k in range(8):
                act(L("ok", 9 * k, 9), L("o", 9 * blk(k), 9), AF.Copy)
            turn(W("ot"), W("ok"))
            dmas([("y", T.old[32 * i:32 * i + r, :], T.ot[0:r, 32 * i:32 * i + 32], [L("ot", 32 * i, 32, 1, 0, r)],
                   [L("old", 0, 32, 1, 32 * i, 32 * i + r)]) for i, r in ((0, 32), (1, 32), (2, 8))])
            dmas([("y", T.ol[:, :], T.old[:, :], [L("old", 0, 32, 1, 0, 72)], [])])
        z = "z%d" % t
        for b in (0, 2, 1, 3):
            if b < 2:
                copy(L(z, b, 288, 4), W("d%d" % b), idx=ll)
            else:
                act(L(z, b, 288, 4), W("d%d" % b), AF.Copy, idx=ll)
        quant(288, z, z)
        for b in range(4):
            mm(1 + b, 288, "w", 128 * b, z)
            act(W("r%d" % b), L("ps%d" % (1 + b), 0, 288), AF.Identity, scale=0.03125)
        for b in range(4):
            tt(L("x%d" % (t + 1), b, 288, 4), W("r%d" % b), W("f%d" % b), A.add, idx=bl)
        products(t + 1)

    for h in range(2):
        mm(5 + h, 144, "v", 0, "x3", 144 * h)
    copy(L("yt", 0, 144), L("ps5", 0, 144))
    act(L("yt", 144, 144), L("ps6", 0, 144), AF.Copy)
    dmas([("y", T.y[:, :], T.yt[:, :], [W("yt")], [])])
    dmas([("y", T.oc[:, :], u8(W("Cx3")), [W("Cx3")], [])]
         + [("s", T.osc[4 * k:4 * k + 4, :], T.Sx3[32 * k:32 * k + 4, 0:288], [W("Sx3")], []) for k in range(4)])

    if not ORDER:
        N = len(ops)
        nxt, left, prio = [[] for _ in ops], [len(o["wait"]) for o in ops], [0.0] * N
        for i, o in enumerate(ops):
            for m in o["wait"]:
                nxt[m].append(i)
        span = lambda o: (o["lat"] if o["q"] else 0.0) or o["dur"]
        for i in reversed(range(N)):
            prio[i] = span(ops[i]) + max([0.0] + [WAKE + prio[k] for k in nxt[i]])
        ready, free, done = {i: 0.0 for i in range(N) if not left[i]}, {q: 0.0 for q in list(queue) + [None]}, [0.0] * N
        while ready:
            begin = {i: max(r, free[ops[i]["q"]]) for i, r in ready.items()}
            first = min(begin, key=lambda i: (begin[i], -prio[i]))
            i = max((k for k in begin if ops[k]["q"] == ops[first]["q"] and begin[k] <= begin[first] + NEAR), key=lambda k: (prio[k], -k))
            o = ops[i]
            at = ready.pop(i)
            if o["q"]:
                free[o["q"]] = begin[i] + o["dur"]
                done[i] = begin[i] + span(o)
            else:
                done[i] = at
            ORDER.append(i)
            for k in nxt[i]:
                left[k] -= 1
                if not left[k]:
                    ready[k] = WAKE + max(done[m] for m in ops[k]["wait"])

    known, total, waited, snap, token = {q: {} for q in queue}, {}, {}, {}, {}
    for i in ORDER:
        o = ops[i]
        q, sem = o["q"], o["sem"]
        if q is None:
            total[sem], token[i] = o["inc"], (sem, o["inc"])
            continue
        want = {}
        for m in o["wait"]:
            s, v = token[m]
            want[s] = max(want.get(s, 0), v)
        for s, v in sorted(want.items(), key=lambda kv: -kv[1]):
            if known[q].get(s, 0) >= v:
                continue
            queue[q].wait_ge(T.sem[s], v)
            waited[s] = max(waited.get(s, 0), v)
            known[q][s] = v
            for s2, v2 in snap.get((s, v), {}).items():
                known[q][s2] = max(known[q].get(s2, 0), v2)
        o["call"]()
        total[sem] = total.get(sem, 0) + 1 if not o["lat"] else o["inc"]
        token[i] = (sem, total[sem])
        seen = snap.setdefault(token[i], {})
        for s2, v2 in known[q].items():
            seen[s2] = max(seen.get(s2, 0), v2)
    for sem in sorted(total):
        if waited.get(sem, 0) < total[sem]:
            g.sync.wait_ge(T.sem[sem], total[sem])
